import numpy as np
import ml_dtypes


def mxq(x, axis, fmt="e4m3"):
    dtype, down = {"e4m3": (ml_dtypes.float8_e4m3fn, 7), "e5m2": (ml_dtypes.float8_e5m2, 14)}[fmt]
    v = np.moveaxis(np.asarray(x, np.float32).astype(ml_dtypes.bfloat16).astype(np.float64), axis, -1)
    blocks = v.reshape(v.shape[:-1] + (-1, 32))
    amax = np.abs(blocks).max(-1, keepdims=True)
    byte = np.maximum(np.where(amax > 0, np.frexp(amax)[1] - 1 + 127, 0) - down, 1)
    scale = np.exp2(byte - 127.0)
    codes = (blocks / scale).astype(np.float32).astype(dtype).astype(np.float64)
    return np.moveaxis((codes * scale).reshape(v.shape), -1, axis)


WIDE = False


def mx_kscale(k):
    if not WIDE:
        return np.ones(k)
    levels = np.array([10, -10, 5, -5, 0])
    if k % 512:
        return np.exp2(np.random.permutation(np.resize(levels, k // 32))).repeat(32)
    a = np.empty((k // 512, 16))
    for p in range(k // 512):
        a[p, :8] = np.random.permutation(np.resize(levels, 8))
        for g in range(8):
            far = levels[np.abs(levels - a[p, g]) >= 10]
            a[p, g + 8] = far[np.random.randint(len(far))]
    return np.exp2(a.ravel()).repeat(32)


def f64(x):
    return np.asarray(x).astype(np.float64)


def striped(idx):
    return np.tile(idx.reshape(-1, 16).T, (8, 1)).astype(np.uint16)


def unstriped(offs):
    return offs[:16].T.reshape(-1).astype(np.int64)


def striped8(idx):
    return np.concatenate([x.reshape(-1, 16).T for x in idx]).astype(np.uint16)


def runs(offs, k):
    lists = np.stack([offs[16 * r : 16 * r + 16].T.reshape(-1) for r in range(8)]).astype(np.int64)
    return lists[np.arange(k) % 512 // 64]


def pack_weight(w):
    k, n = w.shape
    w = f64(np.asarray(w, np.float32).astype(ml_dtypes.bfloat16)).reshape(k // 32, 32, n)
    amax = np.abs(w).max(1)
    byte = np.clip(np.where(amax > 0, np.frexp(amax)[1] - 1 + 127 - 7, 1), 1, 254)
    scaled = (w * np.exp2(127.0 - byte)[:, None, :]).reshape(k, n).astype(np.float32)
    words = np.ascontiguousarray(scaled.reshape(k // 512, 128, 4, n).transpose(0, 1, 3, 2)).astype(ml_dtypes.float8_e4m3fn).view(np.uint8)
    return words, np.ascontiguousarray(byte.astype(np.uint8).reshape(k // 512, 16, n))


def unpack_weight(words, scales):
    g, p, n, _ = words.shape
    vals = np.ascontiguousarray(words).view(ml_dtypes.float8_e4m3fn).astype(np.float64) * np.repeat(np.exp2(scales.astype(np.float64) - 127.0), 8, axis=1)[..., None]
    return vals.transpose(0, 1, 3, 2).reshape(g * 512, n)


E2M1 = np.array([0.0, 0.5, 1.0, 1.5, 2.0, 3.0, 4.0, 6.0, -0.0, -0.5, -1.0, -1.5, -2.0, -3.0, -4.0, -6.0])


def pack_fp4(w):
    k, n = w.shape
    w = f64(np.asarray(w, np.float32).astype(ml_dtypes.bfloat16)).reshape(k // 32, 32, n)
    amax = np.abs(w).max(1)
    mant, ex = np.frexp(amax / 6.0)
    byte = np.clip(np.where(amax > 0, np.where(mant > 0.5, ex, ex - 1) + 127, 1), 1, 254)
    scaled = (w * np.exp2(127.0 - byte)[:, None, :]).reshape(k, n).astype(np.float32)
    c = np.ascontiguousarray(scaled.reshape(k // 512, 128, 4, n).transpose(0, 1, 3, 2)).astype(ml_dtypes.float4_e2m1fn).view(np.uint8) & 0xF
    words = (c[..., 0::2] | (c[..., 1::2] << 4)).reshape(k // 512, 128, 2 * n)
    return np.ascontiguousarray(words), np.ascontiguousarray(byte.astype(np.uint8).reshape(k // 512, 16, n))


def unpack_fp4(words, scales):
    g, _, n = scales.shape
    words = np.ascontiguousarray(words).reshape(g, 128, n, 2)
    nib = np.empty((g, 128, n, 4), np.uint8)
    nib[..., 0::2] = words & 0xF
    nib[..., 1::2] = words >> 4
    vals = E2M1[nib] * np.repeat(np.exp2(scales.astype(np.float64) - 127.0), 8, axis=1)[..., None]
    return vals.transpose(0, 1, 3, 2).reshape(g * 512, n)


K, T, S, H, G = 512, 2048, 256, 512, 2048


def setup_inputs():
    n = np.random.standard_normal
    s = mx_kscale(K)[:, None]
    packed_xT = pack_weight(n((K, T)) * s)
    packed_w1 = pack_fp4(n((K, H)) / np.sqrt(K) / s)
    packed_dT = pack_weight(n((K, G)) / s)
    return {
        "x_words": packed_xT[0],
        "x_scales": packed_xT[1],
        "w1_words": packed_w1[0],
        "w1_scales": packed_w1[1],
        "gs": (np.random.uniform(0.5, 1.5, (K, 1)) * s).astype(np.float32),
        "d_words": packed_dT[0],
        "d_scales": packed_dT[1],
        "offs": striped(np.random.permutation(T)[:S]),
        "ka": striped8(np.random.randint(0, G, (8, H))),
        "kb": striped8(np.random.randint(0, G, (8, H))),
        "n1": striped(np.random.permutation(S)),
        "n2": striped(np.random.permutation(S)),
    }


def reference(x_words, x_scales, w1_words, w1_scales, gs, d_words, d_scales, offs, ka, kb, n1, n2):
    d_ka = unpack_weight(d_words, d_scales)[np.arange(K)[:, None], runs(ka, K)]
    xq = unpack_weight(x_words, x_scales)[:, unstriped(offs)]
    y = unpack_fp4(w1_words, w1_scales).T @ xq
    z = f64(gs) * y
    zq = mxq(z, 0, "e4m3")
    d_kb = unpack_weight(d_words, d_scales)[np.arange(K)[:, None], runs(kb, K)]
    h = 0.0625 * (d_ka.T @ zq + d_kb.T @ zq)
    ds = np.zeros((H, S))
    ds[:, unstriped(n1)] = h
    ds2 = np.zeros((H, S))
    ds2[:, unstriped(n2)] = h
    return np.maximum(ds, ds2)

@@ -1,0 +1,191 @@
+from contextlib import ExitStack
+
+import concourse.mybir as mybir
+
+K, T, S, H, G = 512, 2048, 256, 512, 2048
+FLOPS = 2 * K * H * S * 3
+
+F32 = mybir.dt.float32
+BF16 = mybir.dt.bfloat16
+I32 = mybir.dt.int32
+U32 = mybir.dt.uint32
+U16 = mybir.dt.uint16
+U8 = mybir.dt.uint8
+FP8X4 = mybir.dt.float8_e4m3fn_x4
+FP4X4 = mybir.dt.float4_e2m1fn_x4
+COPY = mybir.ActivationFunctionType.Copy
+MULT = mybir.AluOpType.mult
+MAX = mybir.AluOpType.max
+
+P = 128
+HALF = 128
+PIECE = 256
+
+
+def tile_picked_daqisendtwo_none_p_kernel(
+    tc, x_words, x_scales, w1_words, w1_scales, gs, d_words, d_scales, offs, ka, kb, n1, n2, out
+):
+    nc = tc.nc
+    with ExitStack() as ctx:
+        sb = ctx.enter_context(tc.tile_pool(name="sb", bufs=1))
+        ps = ctx.enter_context(tc.psum_pool(name="ps", bufs=1))
+
+        ka_t = sb.tile([P, H // 16], U16, name="ka_t")
+        kb_t = sb.tile([P, H // 16], U16, name="kb_t")
+        offs_t = sb.tile([P, S // 16], U16, name="offs_t")
+        n1_t = sb.tile([P, S // 16], U16, name="n1_t")
+        n2_t = sb.tile([P, S // 16], U16, name="n2_t")
+        xw = sb.tile([P, T], U32, name="xw")
+        dw = sb.tile([P, G], U32, name="dw")
+        xs = sb.tile([P, T], U8, name="xs")
+        ds = sb.tile([P, G], U8, name="ds")
+        w1w = sb.tile([P, 2 * H], U8, name="w1w")
+        w1s = sb.tile([P, H], U8, name="w1s", tag="bytes", align_bytes=64)
+        gain = sb.tile([P, 4], F32, name="gain")
+
+        nc.vector.memset(ds[:].bitcast(I32), 0)
+        nc.vector.memset(xs[:].bitcast(I32), 0)
+        nc.vector.memset(w1s[:].bitcast(I32), 0)
+
+        nc.sync.dma_start(ka_t[:], ka)
+        nc.sync.dma_start(kb_t[:], kb)
+        nc.sync.dma_start(offs_t[:], offs)
+        nc.sync.dma_start(n1_t[:], n1)
+        nc.sync.dma_start(n2_t[:], n2)
+        nc.scalar.dma_start(ds[0:P:8, :].bitcast(I32), d_scales[0].bitcast(I32))
+        nc.scalar.dma_start(xs[0:P:8, :].bitcast(I32), x_scales[0].bitcast(I32))
+        nc.scalar.dma_start(w1s[0:P:8, :].bitcast(I32), w1_scales[0].bitcast(I32))
+        nc.sync.dma_start(xw[:].bitcast(I32), x_words[0].rearrange("p n t -> p (n t)").bitcast(I32))
+        nc.sync.dma_start(dw[:].bitcast(I32), d_words[0].rearrange("p n t -> p (n t)").bitcast(I32))
+        nc.gpsimd.dma_start(w1w[:].bitcast(I32), w1_words[0].bitcast(I32))
+        nc.gpsimd.dma_start(gain[:], gs.rearrange("(p t) o -> p (t o)", t=4))
+
+        def piece(lst, u):
+            return lst[:, u * (PIECE // 16) : (u + 1) * (PIECE // 16)]
+
+        def settle(planes, queues):
+            for r in (1, 2, 3):
+                queues[r - 1].dma_start(planes[r:P:32, :].bitcast(I32), planes[8 * r : P : 32, :].bitcast(I32))
+
+        got0 = sb.tile([P, 2 * PIECE], U8, name="got0", tag="early", align_bytes=64)
+        gotx = sb.tile([P, PIECE], U8, name="gotx", tag="early2")
+        nc.vector.tensor_copy(got0[:, 0:PIECE], ds[:].indirect(piece(ka_t, 0)))
+        nc.vector.tensor_copy(got0[:, PIECE : 2 * PIECE], ds[:].indirect(piece(kb_t, 0)))
+        nc.vector.tensor_copy(gotx[:], xs[:].indirect(offs_t[:]))
+        planes0 = sb.tile([P, 3 * PIECE + H], U8, name="planes0", align_bytes=64)
+        nc.vector.tensor_copy(
+            planes0[:, 3 * PIECE :].rearrange("p (t m) -> p t m", t=4), w1s[:].rearrange("p (m t) -> p t m", t=4)
+        )
+        nc.vector.tensor_copy(planes0[:, 0 : 2 * PIECE].bitcast(I32), got0[:].bitcast(I32))
+        nc.vector.tensor_copy(planes0[:, 2 * PIECE : 3 * PIECE].bitcast(I32), gotx[:].bitcast(I32))
+        settle(planes0, (nc.sync, nc.scalar, nc.sync))
+
+        w1d = sb.tile([P, 2 * H], U8, name="w1d", align_bytes=64)
+        nc.scalar.copy(
+            w1d[:].bitcast(U16).rearrange("p (t m) -> p t m", t=4),
+            w1w[:].bitcast(U16).rearrange("p (m t) -> p t m", t=4),
+        )
+        xg = sb.tile([P, S], U32, name="xg", tag="early", align_bytes=64)
+        nc.vector.tensor_copy(xg[:], xw[:].indirect(offs_t[:]))
+
+        zq = sb.tile([P, S], U32, name="zq", align_bytes=64)
+        zs = sb.tile([P, S], U8, name="zs", align_bytes=64)
+        x0 = 2 * PIECE
+        w0 = 3 * PIECE
+
+        def first_product(half):
+            y = ps.tile([P, 4, HALF], F32, name="y%d" % half)
+            cols = slice(half * HALF, (half + 1) * HALF)
+            for t in range(4):
+                nc.tensor.matmul_mx(
+                    out=y[:, t, :],
+                    lhsT=w1d[:, 2 * P * t : 2 * P * (t + 1)].bitcast(FP4X4),
+                    lhsT_scale=planes0[:, w0 + P * t : w0 + P * (t + 1)],
+                    rhs=xg[:, cols].bitcast(FP8X4),
+                    rhs_scale=planes0[:, x0 + half * HALF : x0 + (half + 1) * HALF],
+                    start=True,
+                    stop=True,
+                )
+            return y
+
+        def weigh(half, y):
+            zb = sb.tile([P, HALF, 4], BF16, name="zb%d" % half, tag="late", align_bytes=64)
+            nc.vector.tensor_tensor(
+                zb[:], y[:].rearrange("p t n -> p n t"), gain[:].unsqueeze(1).to_broadcast([P, HALF, 4]), MULT
+            )
+            return zb
+
+        def quantise(half, zb):
+            cols = slice(half * HALF, (half + 1) * HALF)
+            nc.vector.quantize_mx(
+                out=zq[:, cols].bitcast(FP8X4), scales=zs[:, cols], in_=zb[:].rearrange("p n t -> p (n t)")
+            )
+
+        def pick_words(u, tag):
+            words = sb.tile([P, 2 * PIECE], U32, name="dg%d" % u, tag=tag, align_bytes=64)
+            for i, lst in enumerate((ka_t, kb_t)):
+                nc.vector.tensor_copy(words[:, i * PIECE : (i + 1) * PIECE], dw[:].indirect(piece(lst, u)))
+            return words
+
+        def second_product(block, cols, words, planes):
+            n = cols.stop - cols.start
+            acc = ps.tile([P, n], F32, name="acc%d_%d" % (block, cols.start))
+            m0 = (block % 2) * P
+            for i in range(2):
+                nc.tensor.matmul_mx(
+                    out=acc[:],
+                    lhsT=words[:, i * PIECE + m0 : i * PIECE + m0 + P].bitcast(FP8X4),
+                    lhsT_scale=planes[:, i * PIECE + m0 : i * PIECE + m0 + P],
+                    rhs=zq[:, cols].bitcast(FP8X4),
+                    rhs_scale=zs[:, cols],
+                    start=(i == 0),
+                    stop=(i == 1),
+                )
+            return acc
+
+        hs = [sb.tile([P, S], F32, name="h%d" % b) for b in range(4)]
+        sent = [[sb.tile([P, 2 * S], F32, name="sent%d_%d" % (b, i)) for i in range(2)] for b in range(4)]
+
+        def send(block, cols):
+            for i, lst in enumerate((n1_t, n2_t)):
+                nc.scalar.activation(
+                    sent[block][i][:].indirect(lst[:, cols.start // 16 : cols.stop // 16]), hs[block][:, cols], COPY
+                )
+
+        def finish(block):
+            res = sb.tile([P, S], F32, name="res%d" % block)
+            nc.vector.tensor_tensor(res[:], sent[block][0][:, 0:S], sent[block][1][:, 0:S], MAX)
+            nc.sync.dma_start(out[block * P : (block + 1) * P, :], res[:])
+
+        lo, hi, both = slice(0, HALF), slice(HALF, S), slice(0, S)
+
+        got1 = sb.tile([P, 2 * PIECE], U8, name="got1", tag="early2")
+        nc.vector.tensor_copy(got1[:, 0:PIECE], ds[:].indirect(piece(ka_t, 1)))
+        nc.vector.tensor_copy(got1[:, PIECE : 2 * PIECE], ds[:].indirect(piece(kb_t, 1)))
+        planes1 = sb.tile([P, 2 * PIECE], U8, name="planes1", align_bytes=64)
+        nc.vector.tensor_copy(planes1[:].bitcast(I32), got1[:].bitcast(I32))
+        settle(planes1, (nc.sync, nc.sync, nc.sync))
+        y0 = first_product(0)
+        y1 = first_product(1)
+        zb0 = weigh(0, y0)
+        words0 = pick_words(0, "bytes")
+        quantise(0, zb0)
+        acc = second_product(0, lo, words0, planes0)
+        nc.scalar.activation(hs[0][:, lo], acc[:], COPY, scale=0.0625)
+        send(0, lo)
+        acc = second_product(1, lo, words0, planes0)
+        nc.vector.tensor_scalar(hs[1][:, lo], acc[:], 0.0625, None, MULT)
+        send(1, lo)
+        zb1 = weigh(1, y1)
+        quantise(1, zb1)
+        for b in (0, 1):
+            acc = second_product(b, hi, words0, planes0)
+            nc.vector.tensor_scalar(hs[b][:, hi], acc[:], 0.0625, None, MULT)
+            send(b, hi)
+        words1 = pick_words(1, "late")
+        for b in (2, 3):
+            acc = second_product(b, both, words1, planes1)
+            nc.vector.tensor_scalar(hs[b][:], acc[:], 0.0625, None, MULT)
+            send(b, both)
+        for b in range(4):
+            finish(b)

@@ -20,6 +20,7 @@ MAX = mybir.AluOpType.max
 P = 128
 HALF = 128
 PIECE = 256
+D_HEAD = 576
 
 
 def tile_picked_daqisendtwo_none_p_kernel(
@@ -28,6 +29,7 @@ def tile_picked_daqisendtwo_none_p_kernel(
     nc = tc.nc
     with ExitStack() as ctx:
         sb = ctx.enter_context(tc.tile_pool(name="sb", bufs=1))
+        turn = ctx.enter_context(tc.tile_pool(name="turn", bufs=1))
         ps = ctx.enter_context(tc.psum_pool(name="ps", bufs=1))
 
         ka_t = sb.tile([P, H // 16], U16, name="ka_t")
@@ -35,63 +37,64 @@ def tile_picked_daqisendtwo_none_p_kernel(
         offs_t = sb.tile([P, S // 16], U16, name="offs_t")
         n1_t = sb.tile([P, S // 16], U16, name="n1_t")
         n2_t = sb.tile([P, S // 16], U16, name="n2_t")
-        xw = sb.tile([P, T], U32, name="xw")
+        xw = turn.tile([P, T], U32, name="xw", align_bytes=64, offset=4096)
         dw = sb.tile([P, G], U32, name="dw")
         xs = sb.tile([P, T], U8, name="xs")
         ds = sb.tile([P, G], U8, name="ds")
         w1w = sb.tile([P, 2 * H], U8, name="w1w")
-        w1s = sb.tile([P, H], U8, name="w1s", tag="bytes", align_bytes=64)
+        w1s = sb.tile([P, H], U8, name="w1s")
         gain = sb.tile([P, 4], F32, name="gain")
 
-        nc.vector.memset(ds[:].bitcast(I32), 0)
-        nc.vector.memset(xs[:].bitcast(I32), 0)
         nc.vector.memset(w1s[:].bitcast(I32), 0)
+        nc.vector.memset(xs[:].bitcast(I32), 0)
+        nc.gpsimd.memset(ds[:].bitcast(I32), 0)
 
+        d_rows = d_words[0].rearrange("p n t -> p (n t)").bitcast(I32)
+        nc.sync.dma_start(dw[:, 0:D_HEAD].bitcast(I32), d_rows[:, 0:D_HEAD])
         nc.sync.dma_start(ka_t[:], ka)
         nc.sync.dma_start(kb_t[:], kb)
         nc.sync.dma_start(offs_t[:], offs)
+        nc.scalar.dma_start(w1s[0:P:8, :].bitcast(I32), w1_scales[0].bitcast(I32))
+        nc.scalar.dma_start(ds[0:P:8, :].bitcast(I32), d_scales[0].bitcast(I32))
+        nc.sync.dma_start(xs[0:P:8, :].bitcast(I32), x_scales[0].bitcast(I32))
+        nc.sync.dma_start(xw[:].bitcast(I32), x_words[0].rearrange("p n t -> p (n t)").bitcast(I32))
+        nc.sync.dma_start(w1w[:].bitcast(I32), w1_words[0].bitcast(I32))
+        nc.sync.dma_start(gain[:], gs.rearrange("(p t) o -> p (t o)", t=4))
+        nc.sync.dma_start(dw[:, D_HEAD:].bitcast(I32), d_rows[:, D_HEAD:])
         nc.sync.dma_start(n1_t[:], n1)
         nc.sync.dma_start(n2_t[:], n2)
-        nc.scalar.dma_start(ds[0:P:8, :].bitcast(I32), d_scales[0].bitcast(I32))
-        nc.scalar.dma_start(xs[0:P:8, :].bitcast(I32), x_scales[0].bitcast(I32))
-        nc.scalar.dma_start(w1s[0:P:8, :].bitcast(I32), w1_scales[0].bitcast(I32))
-        nc.sync.dma_start(xw[:].bitcast(I32), x_words[0].rearrange("p n t -> p (n t)").bitcast(I32))
-        nc.sync.dma_start(dw[:].bitcast(I32), d_words[0].rearrange("p n t -> p (n t)").bitcast(I32))
-        nc.gpsimd.dma_start(w1w[:].bitcast(I32), w1_words[0].bitcast(I32))
-        nc.gpsimd.dma_start(gain[:], gs.rearrange("(p t) o -> p (t o)", t=4))
 
         def piece(lst, u):
             return lst[:, u * (PIECE // 16) : (u + 1) * (PIECE // 16)]
 
-        def settle(planes, queues):
+        def settle(planes):
             for r in (1, 2, 3):
-                queues[r - 1].dma_start(planes[r:P:32, :].bitcast(I32), planes[8 * r : P : 32, :].bitcast(I32))
+                nc.sync.dma_start(planes[r:P:32, :].bitcast(I32), planes[8 * r : P : 32, :].bitcast(I32))
 
-        got0 = sb.tile([P, 2 * PIECE], U8, name="got0", tag="early", align_bytes=64)
-        gotx = sb.tile([P, PIECE], U8, name="gotx", tag="early2")
-        nc.vector.tensor_copy(got0[:, 0:PIECE], ds[:].indirect(piece(ka_t, 0)))
-        nc.vector.tensor_copy(got0[:, PIECE : 2 * PIECE], ds[:].indirect(piece(kb_t, 0)))
-        nc.vector.tensor_copy(gotx[:], xs[:].indirect(offs_t[:]))
-        planes0 = sb.tile([P, 3 * PIECE + H], U8, name="planes0", align_bytes=64)
+        def pick_bytes(u, got):
+            for i, lst in enumerate((ka_t, kb_t)):
+                nc.vector.tensor_copy(got[:, i * PIECE : (i + 1) * PIECE], ds[:].indirect(piece(lst, u)))
+
+        x0 = 2 * PIECE
+        w0 = x0 + S
+        planes0 = sb.tile([P, w0 + H], U8, name="planes0", align_bytes=64)
         nc.vector.tensor_copy(
-            planes0[:, 3 * PIECE :].rearrange("p (t m) -> p t m", t=4), w1s[:].rearrange("p (m t) -> p t m", t=4)
+            planes0[:, w0:].rearrange("p (t m) -> p t m", t=4), w1s[:].rearrange("p (m t) -> p t m", t=4)
         )
-        nc.vector.tensor_copy(planes0[:, 0 : 2 * PIECE].bitcast(I32), got0[:].bitcast(I32))
-        nc.vector.tensor_copy(planes0[:, 2 * PIECE : 3 * PIECE].bitcast(I32), gotx[:].bitcast(I32))
-        settle(planes0, (nc.sync, nc.scalar, nc.sync))
+        got0 = sb.tile([P, w0], U8, name="got0", tag="early", align_bytes=64)
+        pick_bytes(0, got0)
+        nc.vector.tensor_copy(got0[:, x0:], xs[:].indirect(offs_t[:]))
+        nc.vector.tensor_copy(planes0[:, 0:w0].bitcast(I32), got0[:].bitcast(I32))
+        settle(planes0)
 
-        w1d = sb.tile([P, 2 * H], U8, name="w1d", align_bytes=64)
-        nc.scalar.copy(
-            w1d[:].bitcast(U16).rearrange("p (t m) -> p t m", t=4),
-            w1w[:].bitcast(U16).rearrange("p (m t) -> p t m", t=4),
-        )
+        w1d = [sb.tile([P, 2 * P], U8, name="w1d%d" % t, align_bytes=64) for t in range(4)]
+        for t in range(4):
+            nc.scalar.copy(w1d[t][:].bitcast(U16), w1w[:].bitcast(U16)[:, t:H:4])
         xg = sb.tile([P, S], U32, name="xg", tag="early", align_bytes=64)
         nc.vector.tensor_copy(xg[:], xw[:].indirect(offs_t[:]))
 
         zq = sb.tile([P, S], U32, name="zq", align_bytes=64)
         zs = sb.tile([P, S], U8, name="zs", align_bytes=64)
-        x0 = 2 * PIECE
-        w0 = 3 * PIECE
 
         def first_product(half):
             y = ps.tile([P, 4, HALF], F32, name="y%d" % half)
@@ -99,17 +102,17 @@ def tile_picked_daqisendtwo_none_p_kernel(
             for t in range(4):
                 nc.tensor.matmul_mx(
                     out=y[:, t, :],
-                    lhsT=w1d[:, 2 * P * t : 2 * P * (t + 1)].bitcast(FP4X4),
+                    lhsT=w1d[t][:].bitcast(FP4X4),
                     lhsT_scale=planes0[:, w0 + P * t : w0 + P * (t + 1)],
                     rhs=xg[:, cols].bitcast(FP8X4),
-                    rhs_scale=planes0[:, x0 + half * HALF : x0 + (half + 1) * HALF],
+                    rhs_scale=planes0[:, x0 + cols.start : x0 + cols.stop],
                     start=True,
                     stop=True,
                 )
             return y
 
         def weigh(half, y):
-            zb = sb.tile([P, HALF, 4], BF16, name="zb%d" % half, tag="late", align_bytes=64)
+            zb = sb.tile([P, HALF, 4], BF16, name="zb%d" % half, tag="zb", align_bytes=64)
             nc.vector.tensor_tensor(
                 zb[:], y[:].rearrange("p t n -> p n t"), gain[:].unsqueeze(1).to_broadcast([P, HALF, 4]), MULT
             )
@@ -121,15 +124,12 @@ def tile_picked_daqisendtwo_none_p_kernel(
                 out=zq[:, cols].bitcast(FP8X4), scales=zs[:, cols], in_=zb[:].rearrange("p n t -> p (n t)")
             )
 
-        def pick_words(u, tag):
-            words = sb.tile([P, 2 * PIECE], U32, name="dg%d" % u, tag=tag, align_bytes=64)
-            for i, lst in enumerate((ka_t, kb_t)):
-                nc.vector.tensor_copy(words[:, i * PIECE : (i + 1) * PIECE], dw[:].indirect(piece(lst, u)))
-            return words
+        def pick_words(u, i, words):
+            nc.vector.tensor_copy(words[:, i * PIECE : (i + 1) * PIECE], dw[:].indirect(piece((ka_t, kb_t)[i], u)))
 
         def second_product(block, cols, words, planes):
             n = cols.stop - cols.start
-            acc = ps.tile([P, n], F32, name="acc%d_%d" % (block, cols.start))
+            acc = ps.tile([P, n], F32, name="acc%d_%d" % (block, cols.start), tag="acc%d_%d" % (block, cols.start))
             m0 = (block % 2) * P
             for i in range(2):
                 nc.tensor.matmul_mx(
@@ -153,36 +153,35 @@ def tile_picked_daqisendtwo_none_p_kernel(
                 )
 
         def finish(block):
-            res = sb.tile([P, S], F32, name="res%d" % block)
+            res = turn.tile([P, S], F32, name="res%d" % block, align_bytes=64, offset=1024 * block)
             nc.vector.tensor_tensor(res[:], sent[block][0][:, 0:S], sent[block][1][:, 0:S], MAX)
             nc.sync.dma_start(out[block * P : (block + 1) * P, :], res[:])
 
         lo, hi, both = slice(0, HALF), slice(HALF, S), slice(0, S)
 
-        got1 = sb.tile([P, 2 * PIECE], U8, name="got1", tag="early2")
-        nc.vector.tensor_copy(got1[:, 0:PIECE], ds[:].indirect(piece(ka_t, 1)))
-        nc.vector.tensor_copy(got1[:, PIECE : 2 * PIECE], ds[:].indirect(piece(kb_t, 1)))
+        got1 = turn.tile([P, 2 * PIECE], U8, name="got1", align_bytes=64, offset=4096)
+        pick_bytes(1, got1)
         planes1 = sb.tile([P, 2 * PIECE], U8, name="planes1", align_bytes=64)
         nc.vector.tensor_copy(planes1[:].bitcast(I32), got1[:].bitcast(I32))
-        settle(planes1, (nc.sync, nc.sync, nc.sync))
+        settle(planes1)
+        words0 = turn.tile([P, 2 * PIECE], U32, name="words0", align_bytes=64, offset=0)
+        pick_words(0, 0, words0)
+        pick_words(0, 1, words0)
+
         y0 = first_product(0)
         y1 = first_product(1)
-        zb0 = weigh(0, y0)
-        words0 = pick_words(0, "bytes")
-        quantise(0, zb0)
+        quantise(0, weigh(0, y0))
         acc = second_product(0, lo, words0, planes0)
         nc.scalar.activation(hs[0][:, lo], acc[:], COPY, scale=0.0625)
         send(0, lo)
-        acc = second_product(1, lo, words0, planes0)
-        nc.vector.tensor_scalar(hs[1][:, lo], acc[:], 0.0625, None, MULT)
-        send(1, lo)
-        zb1 = weigh(1, y1)
-        quantise(1, zb1)
-        for b in (0, 1):
-            acc = second_product(b, hi, words0, planes0)
-            nc.vector.tensor_scalar(hs[b][:, hi], acc[:], 0.0625, None, MULT)
-            send(b, hi)
-        words1 = pick_words(1, "late")
+        quantise(1, weigh(1, y1))
+        for b, cols in ((0, hi), (1, both)):
+            acc = second_product(b, cols, words0, planes0)
+            nc.vector.tensor_scalar(hs[b][:, cols], acc[:], 0.0625, None, MULT)
+            send(b, cols)
+        words1 = turn.tile([P, 2 * PIECE], U32, name="words1", align_bytes=64, offset=0)
+        pick_words(1, 0, words1)
+        pick_words(1, 1, words1)
         for b in (2, 3):
             acc = second_product(b, both, words1, planes1)
             nc.vector.tensor_scalar(hs[b][:], acc[:], 0.0625, None, MULT)

from contextlib import ExitStack

import concourse.mybir as mybir

K, T, S, H, G = 512, 2048, 256, 512, 2048
FLOPS = 2 * K * H * S * 3

F32 = mybir.dt.float32
BF16 = mybir.dt.bfloat16
I32 = mybir.dt.int32
U32 = mybir.dt.uint32
U16 = mybir.dt.uint16
U8 = mybir.dt.uint8
FP8X4 = mybir.dt.float8_e4m3fn_x4
FP4X4 = mybir.dt.float4_e2m1fn_x4
COPY = mybir.ActivationFunctionType.Copy
MULT = mybir.AluOpType.mult
MAX = mybir.AluOpType.max

P = 128
HALF = 128
PIECE = 256
D_HEAD = 576


def tile_picked_daqisendtwo_none_p_kernel(
    tc, x_words, x_scales, w1_words, w1_scales, gs, d_words, d_scales, offs, ka, kb, n1, n2, out
):
    nc = tc.nc
    with ExitStack() as ctx:
        sb = ctx.enter_context(tc.tile_pool(name="sb", bufs=1))
        turn = ctx.enter_context(tc.tile_pool(name="turn", bufs=1))
        ps = ctx.enter_context(tc.psum_pool(name="ps", bufs=1))

        ka_t = sb.tile([P, H // 16], U16, name="ka_t")
        kb_t = sb.tile([P, H // 16], U16, name="kb_t")
        offs_t = sb.tile([P, S // 16], U16, name="offs_t")
        n1_t = sb.tile([P, S // 16], U16, name="n1_t")
        n2_t = sb.tile([P, S // 16], U16, name="n2_t")
        xw = turn.tile([P, T], U32, name="xw", align_bytes=64, offset=4096)
        dw = sb.tile([P, G], U32, name="dw")
        xs = sb.tile([P, T], U8, name="xs")
        ds = sb.tile([P, G], U8, name="ds")
        w1w = sb.tile([P, 2 * H], U8, name="w1w")
        w1s = sb.tile([P, H], U8, name="w1s")
        gain = sb.tile([P, 4], F32, name="gain")

        nc.vector.memset(w1s[:].bitcast(I32), 0)
        nc.vector.memset(xs[:].bitcast(I32), 0)
        nc.gpsimd.memset(ds[:].bitcast(I32), 0)

        d_rows = d_words[0].rearrange("p n t -> p (n t)").bitcast(I32)
        nc.sync.dma_start(dw[:, 0:D_HEAD].bitcast(I32), d_rows[:, 0:D_HEAD])
        nc.sync.dma_start(ka_t[:], ka)
        nc.sync.dma_start(kb_t[:], kb)
        nc.sync.dma_start(offs_t[:], offs)
        nc.scalar.dma_start(w1s[0:P:8, :].bitcast(I32), w1_scales[0].bitcast(I32))
        nc.scalar.dma_start(ds[0:P:8, :].bitcast(I32), d_scales[0].bitcast(I32))
        nc.sync.dma_start(xs[0:P:8, :].bitcast(I32), x_scales[0].bitcast(I32))
        nc.sync.dma_start(xw[:].bitcast(I32), x_words[0].rearrange("p n t -> p (n t)").bitcast(I32))
        nc.sync.dma_start(w1w[:].bitcast(I32), w1_words[0].bitcast(I32))
        nc.sync.dma_start(gain[:], gs.rearrange("(p t) o -> p (t o)", t=4))
        nc.sync.dma_start(dw[:, D_HEAD:].bitcast(I32), d_rows[:, D_HEAD:])
        nc.sync.dma_start(n1_t[:], n1)
        nc.sync.dma_start(n2_t[:], n2)

        def piece(lst, u):
            return lst[:, u * (PIECE // 16) : (u + 1) * (PIECE // 16)]

        def settle(planes):
            for r in (1, 2, 3):
                nc.sync.dma_start(planes[r:P:32, :].bitcast(I32), planes[8 * r : P : 32, :].bitcast(I32))

        def pick_bytes(u, got):
            for i, lst in enumerate((ka_t, kb_t)):
                nc.vector.tensor_copy(got[:, i * PIECE : (i + 1) * PIECE], ds[:].indirect(piece(lst, u)))

        x0 = 2 * PIECE
        w0 = x0 + S
        planes0 = sb.tile([P, w0 + H], U8, name="planes0", align_bytes=64)
        nc.vector.tensor_copy(
            planes0[:, w0:].rearrange("p (t m) -> p t m", t=4), w1s[:].rearrange("p (m t) -> p t m", t=4)
        )
        got0 = sb.tile([P, w0], U8, name="got0", tag="early", align_bytes=64)
        pick_bytes(0, got0)
        nc.vector.tensor_copy(got0[:, x0:], xs[:].indirect(offs_t[:]))
        nc.vector.tensor_copy(planes0[:, 0:w0].bitcast(I32), got0[:].bitcast(I32))
        settle(planes0)

        w1d = [sb.tile([P, 2 * P], U8, name="w1d%d" % t, align_bytes=64) for t in range(4)]
        for t in range(4):
            nc.scalar.copy(w1d[t][:].bitcast(U16), w1w[:].bitcast(U16)[:, t:H:4])
        xg = sb.tile([P, S], U32, name="xg", tag="early", align_bytes=64)
        nc.vector.tensor_copy(xg[:], xw[:].indirect(offs_t[:]))

        zq = sb.tile([P, S], U32, name="zq", align_bytes=64)
        zs = sb.tile([P, S], U8, name="zs", align_bytes=64)

        def first_product(half):
            y = ps.tile([P, 4, HALF], F32, name="y%d" % half)
            cols = slice(half * HALF, (half + 1) * HALF)
            for t in range(4):
                nc.tensor.matmul_mx(
                    out=y[:, t, :],
                    lhsT=w1d[t][:].bitcast(FP4X4),
                    lhsT_scale=planes0[:, w0 + P * t : w0 + P * (t + 1)],
                    rhs=xg[:, cols].bitcast(FP8X4),
                    rhs_scale=planes0[:, x0 + cols.start : x0 + cols.stop],
                    start=True,
                    stop=True,
                )
            return y

        def weigh(half, y):
            zb = sb.tile([P, HALF, 4], BF16, name="zb%d" % half, tag="zb", align_bytes=64)
            nc.vector.tensor_tensor(
                zb[:], y[:].rearrange("p t n -> p n t"), gain[:].unsqueeze(1).to_broadcast([P, HALF, 4]), MULT
            )
            return zb

        def quantise(half, zb):
            cols = slice(half * HALF, (half + 1) * HALF)
            nc.vector.quantize_mx(
                out=zq[:, cols].bitcast(FP8X4), scales=zs[:, cols], in_=zb[:].rearrange("p n t -> p (n t)")
            )

        def pick_words(u, i, words):
            nc.vector.tensor_copy(words[:, i * PIECE : (i + 1) * PIECE], dw[:].indirect(piece((ka_t, kb_t)[i], u)))

        def second_product(block, cols, words, planes):
            n = cols.stop - cols.start
            acc = ps.tile([P, n], F32, name="acc%d_%d" % (block, cols.start), tag="acc%d_%d" % (block, cols.start))
            m0 = (block % 2) * P
            for i in range(2):
                nc.tensor.matmul_mx(
                    out=acc[:],
                    lhsT=words[:, i * PIECE + m0 : i * PIECE + m0 + P].bitcast(FP8X4),
                    lhsT_scale=planes[:, i * PIECE + m0 : i * PIECE + m0 + P],
                    rhs=zq[:, cols].bitcast(FP8X4),
                    rhs_scale=zs[:, cols],
                    start=(i == 0),
                    stop=(i == 1),
                )
            return acc

        hs = [sb.tile([P, S], F32, name="h%d" % b) for b in range(4)]
        sent = [[sb.tile([P, 2 * S], F32, name="sent%d_%d" % (b, i)) for i in range(2)] for b in range(4)]

        def send(block, cols):
            for i, lst in enumerate((n1_t, n2_t)):
                nc.scalar.activation(
                    sent[block][i][:].indirect(lst[:, cols.start // 16 : cols.stop // 16]), hs[block][:, cols], COPY
                )

        def finish(block):
            res = turn.tile([P, S], F32, name="res%d" % block, align_bytes=64, offset=1024 * block)
            nc.vector.tensor_tensor(res[:], sent[block][0][:, 0:S], sent[block][1][:, 0:S], MAX)
            nc.sync.dma_start(out[block * P : (block + 1) * P, :], res[:])

        lo, hi, both = slice(0, HALF), slice(HALF, S), slice(0, S)

        got1 = turn.tile([P, 2 * PIECE], U8, name="got1", align_bytes=64, offset=4096)
        pick_bytes(1, got1)
        planes1 = sb.tile([P, 2 * PIECE], U8, name="planes1", align_bytes=64)
        nc.vector.tensor_copy(planes1[:].bitcast(I32), got1[:].bitcast(I32))
        settle(planes1)
        words0 = turn.tile([P, 2 * PIECE], U32, name="words0", align_bytes=64, offset=0)
        pick_words(0, 0, words0)
        pick_words(0, 1, words0)

        y0 = first_product(0)
        y1 = first_product(1)
        quantise(0, weigh(0, y0))
        acc = second_product(0, lo, words0, planes0)
        nc.scalar.activation(hs[0][:, lo], acc[:], COPY, scale=0.0625)
        send(0, lo)
        quantise(1, weigh(1, y1))
        for b, cols in ((0, hi), (1, both)):
            acc = second_product(b, cols, words0, planes0)
            nc.vector.tensor_scalar(hs[b][:, cols], acc[:], 0.0625, None, MULT)
            send(b, cols)
        words1 = turn.tile([P, 2 * PIECE], U32, name="words1", align_bytes=64, offset=0)
        pick_words(1, 0, words1)
        pick_words(1, 1, words1)
        for b in (2, 3):
            acc = second_product(b, both, words1, planes1)
            nc.vector.tensor_scalar(hs[b][:], acc[:], 0.0625, None, MULT)
            send(b, both)
        for b in range(4):
            finish(b)
